import numpy as np
import ml_dtypes


def mxq(x, axis, fmt="e4m3"):
    dtype, down = {"e4m3": (ml_dtypes.float8_e4m3fn, 7), "e5m2": (ml_dtypes.float8_e5m2, 14)}[fmt]
    v = np.moveaxis(np.asarray(x, np.float32).astype(ml_dtypes.bfloat16).astype(np.float64), axis, -1)
    blocks = v.reshape(v.shape[:-1] + (-1, 32))
    amax = np.abs(blocks).max(-1, keepdims=True)
    byte = np.maximum(np.where(amax > 0, np.frexp(amax)[1] - 1 + 127, 0) - down, 1)
    scale = np.exp2(byte - 127.0)
    codes = (blocks / scale).astype(np.float32).astype(dtype).astype(np.float64)
    return np.moveaxis((codes * scale).reshape(v.shape), -1, axis)


WIDE = False


def mx_kscale(k):
    if not WIDE:
        return np.ones(k)
    levels = np.array([10, -10, 5, -5, 0])
    if k % 512:
        return np.exp2(np.random.permutation(np.resize(levels, k // 32))).repeat(32)
    a = np.empty((k // 512, 16))
    for p in range(k // 512):
        a[p, :8] = np.random.permutation(np.resize(levels, 8))
        for g in range(8):
            far = levels[np.abs(levels - a[p, g]) >= 10]
            a[p, g + 8] = far[np.random.randint(len(far))]
    return np.exp2(a.ravel()).repeat(32)


def f64(x):
    return np.asarray(x).astype(np.float64)


def striped(idx):
    return np.tile(np.asarray(idx).reshape(-1, 16).T, (8, 1)).astype(np.uint16)


def unstriped(offs):
    return offs[:16].T.reshape(-1).astype(np.int64)


E2M1 = np.array([0.0, 0.5, 1.0, 1.5, 2.0, 3.0, 4.0, 6.0, -0.0, -0.5, -1.0, -1.5, -2.0, -3.0, -4.0, -6.0])


def pack_weight(w, fmt):
    k, n = w.shape
    w = f64(np.asarray(w, np.float32).astype(ml_dtypes.bfloat16)).reshape(k // 32, 32, n)
    amax = np.abs(w).max(1)
    if fmt == "e4m3":
        byte = np.frexp(amax)[1] - 1 + 127 - 7
    else:
        mant, ex = np.frexp(amax / 6.0)
        byte = np.where(mant > 0.5, ex, ex - 1) + 127
    byte = np.clip(np.where(amax > 0, byte, 1), 1, 254)
    scaled = (w * np.exp2(127.0 - byte)[:, None, :]).reshape(k, n).astype(np.float32)
    by_word = np.ascontiguousarray(scaled.reshape(k // 512, 128, 4, n).transpose(0, 1, 3, 2))
    if fmt == "e4m3":
        words = by_word.astype(ml_dtypes.float8_e4m3fn).view(np.uint8)
    else:
        c = by_word.astype(ml_dtypes.float4_e2m1fn).view(np.uint8) & 0xF
        words = (c[..., 0::2] | (c[..., 1::2] << 4)).reshape(k // 512, 128, 2 * n)
    return np.ascontiguousarray(words), np.ascontiguousarray(byte.astype(np.uint8).reshape(k // 512, 16, n))


def unpack_weight(words, scales, fmt):
    g, _, n = scales.shape
    words = np.ascontiguousarray(words).reshape(g, 128, n, -1)
    if fmt == "e4m3":
        vals = words.view(ml_dtypes.float8_e4m3fn).astype(np.float64)
    else:
        nib = np.empty((g, 128, n, 4), np.uint8)
        nib[..., 0::2] = words & 0xF
        nib[..., 1::2] = words >> 4
        vals = E2M1[nib]
    vals = vals * np.repeat(np.exp2(scales.astype(np.float64) - 127.0), 8, axis=1)[..., None]
    return vals.transpose(0, 1, 3, 2).reshape(g * 512, n)


D, T, I, J, U, Z, M, N = 512, 2048, 512, 512, 1024, 1024, 512, 64


def setup_inputs():
    n = np.random.standard_normal
    idx = np.random.permutation(T)[:I]
    idx2 = np.random.permutation(U)[:J]
    idx3 = np.random.permutation(Z)[:J]
    idx4 = np.random.permutation(M)[:N]
    fd = mx_kscale(D)
    keysp = pack_weight(n((D, T)) / fd[:, None], "e4m3")
    return {
        "keys_words": keysp[0],
        "keys_scales": keysp[1],
        "notes": (n((D, U)) * 1.0 / np.sqrt(D) * fd[:, None]).astype(np.float32),
        "given": (np.random.uniform(0.3, 1.7, (I, Z))).astype(np.float32),
        "old": (1.0 * n((I, M))).astype(np.float32),
        "offs": striped(idx),
        "offs2": striped(idx2),
        "offs3": striped(idx3),
        "offs4": striped(idx4),
    }


def reference(keys_words, keys_scales, notes, given, old, offs, offs2, offs3, offs4):
    idx = unstriped(offs)
    idx2 = unstriped(offs2)
    idx3 = unstriped(offs3)
    idx4 = unstriped(offs4)
    keysu = unpack_weight(keys_words, keys_scales, "e4m3")
    keysidxg = keysu[:, idx]
    notesidx2q = mxq(f64(notes)[:, idx2], 0, "e4m3")
    g1 = keysidxg.T @ notesidx2q
    g0 = g1 * f64(given)[:, idx3]
    rb0 = g0.reshape(I, N, J // N).max(axis=2)
    gf = np.zeros((I, M))
    gf[:, idx4] = rb0
    y = f64(old) + gf
    return y

@@ -1,0 +1,128 @@
+from contextlib import ExitStack
+
+import concourse.mybir as mybir
+
+D, T, I, J, U, Z, M, N = 512, 2048, 512, 512, 1024, 1024, 512, 64
+FLOPS = 2 * D * I * J
+
+F32 = mybir.dt.float32
+BF16 = mybir.dt.bfloat16
+I32 = mybir.dt.int32
+U32 = mybir.dt.uint32
+U16 = mybir.dt.uint16
+U8 = mybir.dt.uint8
+FP8X4 = mybir.dt.float8_e4m3fn_x4
+COPY = mybir.ActivationFunctionType.Copy
+ALU = mybir.AluOpType
+
+P = 128
+PACK = 4
+RUN = J // N
+ROW_TILES = I // P
+
+
+def tile_attend_tab_timestable_runsput_kernel(
+    tc, keys_words, keys_scales, notes, given, old, offs, offs2, offs3, offs4, out
+):
+    nc = tc.nc
+    with ExitStack() as ctx:
+        sb = ctx.enter_context(tc.tile_pool(name="sb", bufs=1))
+        psum = ctx.enter_context(tc.psum_pool(name="psum", bufs=1))
+
+        key_list = sb.tile([P, I // 16], U16, name="key_list")
+        note_list = sb.tile([P, J // 16], U16, name="note_list")
+        given_list = sb.tile([P, J // 16], U16, name="given_list")
+        place_list = sb.tile([P, N // 16], U16, name="place_list")
+        nc.sync.dma_start(note_list[:], offs2)
+        nc.sync.dma_start(key_list[:], offs)
+        nc.sync.dma_start(given_list[:], offs3)
+        nc.sync.dma_start(place_list[:], offs4)
+
+        pool_scales = sb.tile([P, T], U8, name="pool_scales", align_bytes=64)
+        nc.vector.memset(pool_scales[:].bitcast(I32), 0)
+        for q in range(4):
+            nc.gpsimd.dma_start(
+                pool_scales[32 * q : 32 * q + 4, :].bitcast(I32),
+                keys_scales[0, 4 * q : 4 * q + 4, :].bitcast(I32),
+            )
+
+        note_rows = notes.rearrange("(p t) u -> t p u", t=PACK)
+        note_planes = []
+        for t in range(PACK):
+            plane = sb.tile([P, U], F32, name=f"note_plane{t}")
+            nc.sync.dma_start(plane[:], note_rows[t])
+            note_planes.append(plane)
+
+        pool_words = sb.tile([P, T], U32, name="pool_words", align_bytes=64)
+        nc.sync.dma_start(
+            pool_words[:].bitcast(I32), keys_words[0].rearrange("p n t -> p (n t)").bitcast(I32)
+        )
+
+        given_rows, old_rows, placed = [], [], []
+        for r in range(ROW_TILES):
+            g = sb.tile([P, Z], F32, name=f"given_rows{r}")
+            nc.sync.dma_start(g[:], given[r * P : (r + 1) * P, :])
+            given_rows.append(g)
+        for r in range(ROW_TILES):
+            o = sb.tile([P, M], F32, name=f"old_rows{r}")
+            nc.sync.dma_start(o[:], old[r * P : (r + 1) * P, :])
+            old_rows.append(o)
+        for r in range(ROW_TILES):
+            z = sb.tile([P, M], F32, name=f"placed{r}")
+            nc.vector.memset(z[:], 0.0)
+            placed.append(z)
+
+        picked_notes = sb.tile([P, PACK, J], BF16, name="picked_notes", align_bytes=64)
+        key_scales = sb.tile([P, I], U8, name="key_scales", align_bytes=64)
+        nc.scalar.activation(picked_notes[:, 0, :], note_planes[0][:].indirect(note_list[:]), COPY)
+        nc.vector.tensor_copy(picked_notes[:, 1, :], note_planes[1][:].indirect(note_list[:]))
+        nc.vector.tensor_copy(key_scales[:], pool_scales[:].indirect(key_list[:]))
+        nc.scalar.activation(picked_notes[:, 2, :], note_planes[2][:].indirect(note_list[:]), COPY)
+        nc.vector.tensor_copy(picked_notes[:, 3, :], note_planes[3][:].indirect(note_list[:]))
+
+        woven = sb.tile([P, J, PACK], BF16, name="woven", align_bytes=64)
+        nc.vector.tensor_copy(
+            woven[:].rearrange("p (c i) t -> p c t i", i=4),
+            picked_notes[:].rearrange("p t (c i) -> p c t i", i=4),
+        )
+        note_words = sb.tile([P, J], U32, name="note_words", align_bytes=64)
+        note_scales = sb.tile([P, J], U8, name="note_scales", align_bytes=64)
+        nc.vector.quantize_mx(
+            out=note_words[:].bitcast(FP8X4),
+            scales=note_scales[:],
+            in_=woven[:].rearrange("p j t -> p (j t)"),
+        )
+
+        key_words = sb.tile([P, I], U32, name="key_words", align_bytes=64)
+        half = I // 2
+        for h in range(2):
+            nc.vector.tensor_copy(
+                key_words[:, h * half : (h + 1) * half],
+                pool_words[:].indirect(key_list[:, h * half // 16 : (h + 1) * half // 16]),
+            )
+
+        for r in range(ROW_TILES):
+            rows = slice(r * P, (r + 1) * P)
+            products = psum.tile([P, J], F32, name=f"products{r}")
+            nc.tensor.matmul_mx(
+                out=products[:],
+                lhsT=key_words[:, rows].bitcast(FP8X4),
+                lhsT_scale=key_scales[:, rows],
+                rhs=note_words[:].bitcast(FP8X4),
+                rhs_scale=note_scales[:],
+                start=True,
+                stop=True,
+            )
+            picked_given = sb.tile([P, J], F32, name=f"picked_given{r}")
+            nc.scalar.activation(picked_given[:], given_rows[r][:].indirect(given_list[:]), COPY)
+            table = sb.tile([P, J], F32, name=f"table{r}")
+            nc.vector.tensor_tensor(table[:], products[:], picked_given[:], ALU.mult)
+            largest = sb.tile([P, N], F32, name=f"largest{r}")
+            nc.vector.tensor_reduce(
+                largest[:], table[:].rearrange("p (n j) -> p n j", j=RUN), mybir.AxisListType.X, ALU.max
+            )
+            nc.scalar.activation(placed[r][:].indirect(place_list[:]), largest[:], COPY)
+            result = sb.tile([P, M], F32, name=f"result{r}")
+            adder = nc.gpsimd if r < 2 else nc.vector
+            adder.tensor_tensor(result[:], old_rows[r][:], placed[r][:], ALU.add)
+            nc.sync.dma_start(out[rows, :], result[:])

@@ -19,6 +19,7 @@ P = 128
 PACK = 4
 RUN = J // N
 ROW_TILES = I // P
+HALF = J // 2
 
 
 def tile_attend_tab_timestable_runsput_kernel(
@@ -35,13 +36,11 @@ def tile_attend_tab_timestable_runsput_kernel(
         place_list = sb.tile([P, N // 16], U16, name="place_list")
         nc.sync.dma_start(note_list[:], offs2)
         nc.sync.dma_start(key_list[:], offs)
-        nc.sync.dma_start(given_list[:], offs3)
-        nc.sync.dma_start(place_list[:], offs4)
 
         pool_scales = sb.tile([P, T], U8, name="pool_scales", align_bytes=64)
-        nc.vector.memset(pool_scales[:].bitcast(I32), 0)
+        nc.gpsimd.memset(pool_scales[:].bitcast(I32), 0)
         for q in range(4):
-            nc.gpsimd.dma_start(
+            nc.scalar.dma_start(
                 pool_scales[32 * q : 32 * q + 4, :].bitcast(I32),
                 keys_scales[0, 4 * q : 4 * q + 4, :].bitcast(I32),
             )
@@ -57,6 +56,8 @@ def tile_attend_tab_timestable_runsput_kernel(
         nc.sync.dma_start(
             pool_words[:].bitcast(I32), keys_words[0].rearrange("p n t -> p (n t)").bitcast(I32)
         )
+        nc.sync.dma_start(given_list[:], offs3)
+        nc.sync.dma_start(place_list[:], offs4)
 
         given_rows, old_rows, placed = [], [], []
         for r in range(ROW_TILES):
@@ -72,37 +73,46 @@ def tile_attend_tab_timestable_runsput_kernel(
             nc.vector.memset(z[:], 0.0)
             placed.append(z)
 
+        def vector_gather(dst, window, offsets):
+            nc.vector.tensor_copy(dst, window[:].indirect(offsets))
+
+        def scalar_gather(dst, window, offsets):
+            nc.scalar.activation(dst, window[:].indirect(offsets), COPY)
+
+        halves = [slice(0, HALF), slice(HALF, 2 * HALF)]
+        list_halves = [slice(0, HALF // 16), slice(HALF // 16, 2 * HALF // 16)]
+
         picked_notes = sb.tile([P, PACK, J], BF16, name="picked_notes", align_bytes=64)
         key_scales = sb.tile([P, I], U8, name="key_scales", align_bytes=64)
-        nc.scalar.activation(picked_notes[:, 0, :], note_planes[0][:].indirect(note_list[:]), COPY)
-        nc.vector.tensor_copy(picked_notes[:, 1, :], note_planes[1][:].indirect(note_list[:]))
-        nc.vector.tensor_copy(key_scales[:], pool_scales[:].indirect(key_list[:]))
-        nc.scalar.activation(picked_notes[:, 2, :], note_planes[2][:].indirect(note_list[:]), COPY)
-        nc.vector.tensor_copy(picked_notes[:, 3, :], note_planes[3][:].indirect(note_list[:]))
+        scalar_gather(picked_notes[:, 0, :], note_planes[0], note_list[:])
+        vector_gather(key_scales[:], pool_scales, key_list[:])
+        vector_gather(picked_notes[:, 1, :], note_planes[1], note_list[:])
+        scalar_gather(picked_notes[:, 2, :], note_planes[2], note_list[:])
+        vector_gather(picked_notes[:, 3, halves[0]], note_planes[3], note_list[:, list_halves[0]])
+        scalar_gather(picked_notes[:, 3, halves[1]], note_planes[3], note_list[:, list_halves[1]])
 
         woven = sb.tile([P, J, PACK], BF16, name="woven", align_bytes=64)
-        nc.vector.tensor_copy(
-            woven[:].rearrange("p (c i) t -> p c t i", i=4),
-            picked_notes[:].rearrange("p t (c i) -> p c t i", i=4),
-        )
+        for h in halves:
+            nc.vector.tensor_copy(
+                woven[:, h, :].rearrange("p (c i) t -> p c t i", i=4),
+                picked_notes[:, :, h].rearrange("p t (c i) -> p c t i", i=4),
+            )
         note_words = sb.tile([P, J], U32, name="note_words", align_bytes=64)
         note_scales = sb.tile([P, J], U8, name="note_scales", align_bytes=64)
-        nc.vector.quantize_mx(
-            out=note_words[:].bitcast(FP8X4),
-            scales=note_scales[:],
-            in_=woven[:].rearrange("p j t -> p (j t)"),
-        )
+        for h in halves:
+            nc.vector.quantize_mx(
+                out=note_words[:, h].bitcast(FP8X4),
+                scales=note_scales[:, h],
+                in_=woven[:, h, :].rearrange("p j t -> p (j t)"),
+            )
 
         key_words = sb.tile([P, I], U32, name="key_words", align_bytes=64)
-        half = I // 2
         for h in range(2):
-            nc.vector.tensor_copy(
-                key_words[:, h * half : (h + 1) * half],
-                pool_words[:].indirect(key_list[:, h * half // 16 : (h + 1) * half // 16]),
-            )
+            vector_gather(key_words[:, halves[h]], pool_words, key_list[:, list_halves[h]])
 
         for r in range(ROW_TILES):
             rows = slice(r * P, (r + 1) * P)
+            last = r == ROW_TILES - 1
             products = psum.tile([P, J], F32, name=f"products{r}")
             nc.tensor.matmul_mx(
                 out=products[:],
@@ -114,15 +124,29 @@ def tile_attend_tab_timestable_runsput_kernel(
                 stop=True,
             )
             picked_given = sb.tile([P, J], F32, name=f"picked_given{r}")
-            nc.scalar.activation(picked_given[:], given_rows[r][:].indirect(given_list[:]), COPY)
+            if r == 0:
+                vector_gather(picked_given[:, halves[0]], given_rows[r], given_list[:, list_halves[0]])
+                scalar_gather(picked_given[:, halves[1]], given_rows[r], given_list[:, list_halves[1]])
+            elif last:
+                for h in range(2):
+                    scalar_gather(picked_given[:, halves[h]], given_rows[r], given_list[:, list_halves[h]])
+            else:
+                scalar_gather(picked_given[:], given_rows[r], given_list[:])
             table = sb.tile([P, J], F32, name=f"table{r}")
-            nc.vector.tensor_tensor(table[:], products[:], picked_given[:], ALU.mult)
             largest = sb.tile([P, N], F32, name=f"largest{r}")
-            nc.vector.tensor_reduce(
-                largest[:], table[:].rearrange("p (n j) -> p n j", j=RUN), mybir.AxisListType.X, ALU.max
-            )
-            nc.scalar.activation(placed[r][:].indirect(place_list[:]), largest[:], COPY)
+            for cols in halves if last else [slice(0, J)]:
+                nc.vector.tensor_tensor(table[:, cols], products[:, cols], picked_given[:, cols], ALU.mult)
+                nc.vector.tensor_reduce(
+                    largest[:, cols.start // RUN : cols.stop // RUN],
+                    table[:, cols].rearrange("p (n j) -> p n j", j=RUN),
+                    mybir.AxisListType.X,
+                    ALU.max,
+                )
+            if r == 2:
+                nc.scalar.activation(placed[r][:].indirect(place_list[:]), largest[:], COPY)
+            else:
+                nc.vector.tensor_copy(placed[r][:].indirect(place_list[:]), largest[:])
             result = sb.tile([P, M], F32, name=f"result{r}")
-            adder = nc.gpsimd if r < 2 else nc.vector
+            adder = nc.vector if last else nc.gpsimd
             adder.tensor_tensor(result[:], old_rows[r][:], placed[r][:], ALU.add)
             nc.sync.dma_start(out[rows, :], result[:])

@@ -39,11 +39,6 @@ def tile_attend_tab_timestable_runsput_kernel(
 
         pool_scales = sb.tile([P, T], U8, name="pool_scales", align_bytes=64)
         nc.gpsimd.memset(pool_scales[:].bitcast(I32), 0)
-        for q in range(4):
-            nc.scalar.dma_start(
-                pool_scales[32 * q : 32 * q + 4, :].bitcast(I32),
-                keys_scales[0, 4 * q : 4 * q + 4, :].bitcast(I32),
-            )
 
         note_rows = notes.rearrange("(p t) u -> t p u", t=PACK)
         note_planes = []
@@ -51,6 +46,12 @@ def tile_attend_tab_timestable_runsput_kernel(
             plane = sb.tile([P, U], F32, name=f"note_plane{t}")
             nc.sync.dma_start(plane[:], note_rows[t])
             note_planes.append(plane)
+            if t == 0:
+                for f in range(4):
+                    nc.sync.dma_start(
+                        pool_scales[f:P:32, :].bitcast(I32),
+                        keys_scales[0, f:16:4, :].bitcast(I32),
+                    )
 
         pool_words = sb.tile([P, T], U32, name="pool_words", align_bytes=64)
         nc.sync.dma_start(
@@ -86,10 +87,9 @@ def tile_attend_tab_timestable_runsput_kernel(
         key_scales = sb.tile([P, I], U8, name="key_scales", align_bytes=64)
         scalar_gather(picked_notes[:, 0, :], note_planes[0], note_list[:])
         vector_gather(key_scales[:], pool_scales, key_list[:])
-        vector_gather(picked_notes[:, 1, :], note_planes[1], note_list[:])
-        scalar_gather(picked_notes[:, 2, :], note_planes[2], note_list[:])
-        vector_gather(picked_notes[:, 3, halves[0]], note_planes[3], note_list[:, list_halves[0]])
-        scalar_gather(picked_notes[:, 3, halves[1]], note_planes[3], note_list[:, list_halves[1]])
+        for t in range(1, PACK):
+            vector_gather(picked_notes[:, t, halves[0]], note_planes[t], note_list[:, list_halves[0]])
+            scalar_gather(picked_notes[:, t, halves[1]], note_planes[t], note_list[:, list_halves[1]])
 
         woven = sb.tile([P, J, PACK], BF16, name="woven", align_bytes=64)
         for h in halves:
@@ -106,9 +106,11 @@ def tile_attend_tab_timestable_runsput_kernel(
                 in_=woven[:, h, :].rearrange("p j t -> p (j t)"),
             )
 
-        key_words = sb.tile([P, I], U32, name="key_words", align_bytes=64)
-        for h in range(2):
-            vector_gather(key_words[:, halves[h]], pool_words, key_list[:, list_halves[h]])
+        first_words = sb.tile([P, P], U32, name="first_words", align_bytes=64)
+        later_words = sb.tile([P, I - P], U32, name="later_words", align_bytes=64)
+        vector_gather(first_words[:], pool_words, key_list[:, : P // 16])
+        vector_gather(later_words[:], pool_words, key_list[:, P // 16 :])
+        key_words = [first_words[:]] + [later_words[:, r * P : (r + 1) * P] for r in range(ROW_TILES - 1)]
 
         for r in range(ROW_TILES):
             rows = slice(r * P, (r + 1) * P)
@@ -116,7 +118,7 @@ def tile_attend_tab_timestable_runsput_kernel(
             products = psum.tile([P, J], F32, name=f"products{r}")
             nc.tensor.matmul_mx(
                 out=products[:],
-                lhsT=key_words[:, rows].bitcast(FP8X4),
+                lhsT=key_words[r].bitcast(FP8X4),
                 lhsT_scale=key_scales[:, rows],
                 rhs=note_words[:].bitcast(FP8X4),
                 rhs_scale=note_scales[:],
@@ -134,19 +136,17 @@ def tile_attend_tab_timestable_runsput_kernel(
                 scalar_gather(picked_given[:], given_rows[r], given_list[:])
             table = sb.tile([P, J], F32, name=f"table{r}")
             largest = sb.tile([P, N], F32, name=f"largest{r}")
-            for cols in halves if last else [slice(0, J)]:
+            for cols in halves:
                 nc.vector.tensor_tensor(table[:, cols], products[:, cols], picked_given[:, cols], ALU.mult)
+            for cols in halves:
                 nc.vector.tensor_reduce(
                     largest[:, cols.start // RUN : cols.stop // RUN],
                     table[:, cols].rearrange("p (n j) -> p n j", j=RUN),
                     mybir.AxisListType.X,
                     ALU.max,
                 )
-            if r == 2:
-                nc.scalar.activation(placed[r][:].indirect(place_list[:]), largest[:], COPY)
-            else:
-                nc.vector.tensor_copy(placed[r][:].indirect(place_list[:]), largest[:])
+            nc.scalar.activation(placed[r][:].indirect(place_list[:]), largest[:], COPY)
             result = sb.tile([P, M], F32, name=f"result{r}")
-            adder = nc.vector if last else nc.gpsimd
+            adder = nc.gpsimd if r < 2 else nc.vector
             adder.tensor_tensor(result[:], old_rows[r][:], placed[r][:], ALU.add)
             nc.sync.dma_start(out[rows, :], result[:])

from contextlib import ExitStack

import concourse.mybir as mybir

D, T, I, J, U, Z, M, N = 512, 2048, 512, 512, 1024, 1024, 512, 64
FLOPS = 2 * D * I * J

F32 = mybir.dt.float32
BF16 = mybir.dt.bfloat16
I32 = mybir.dt.int32
U32 = mybir.dt.uint32
U16 = mybir.dt.uint16
U8 = mybir.dt.uint8
FP8X4 = mybir.dt.float8_e4m3fn_x4
COPY = mybir.ActivationFunctionType.Copy
ALU = mybir.AluOpType

P = 128
PACK = 4
RUN = J // N
ROW_TILES = I // P
HALF = J // 2


def tile_attend_tab_timestable_runsput_kernel(
    tc, keys_words, keys_scales, notes, given, old, offs, offs2, offs3, offs4, out
):
    nc = tc.nc
    with ExitStack() as ctx:
        sb = ctx.enter_context(tc.tile_pool(name="sb", bufs=1))
        psum = ctx.enter_context(tc.psum_pool(name="psum", bufs=1))

        key_list = sb.tile([P, I // 16], U16, name="key_list")
        note_list = sb.tile([P, J // 16], U16, name="note_list")
        given_list = sb.tile([P, J // 16], U16, name="given_list")
        place_list = sb.tile([P, N // 16], U16, name="place_list")
        nc.sync.dma_start(note_list[:], offs2)
        nc.sync.dma_start(key_list[:], offs)

        pool_scales = sb.tile([P, T], U8, name="pool_scales", align_bytes=64)
        nc.gpsimd.memset(pool_scales[:].bitcast(I32), 0)

        note_rows = notes.rearrange("(p t) u -> t p u", t=PACK)
        note_planes = []
        for t in range(PACK):
            plane = sb.tile([P, U], F32, name=f"note_plane{t}")
            nc.sync.dma_start(plane[:], note_rows[t])
            note_planes.append(plane)
            if t == 0:
                for f in range(4):
                    nc.sync.dma_start(
                        pool_scales[f:P:32, :].bitcast(I32),
                        keys_scales[0, f:16:4, :].bitcast(I32),
                    )

        pool_words = sb.tile([P, T], U32, name="pool_words", align_bytes=64)
        nc.sync.dma_start(
            pool_words[:].bitcast(I32), keys_words[0].rearrange("p n t -> p (n t)").bitcast(I32)
        )
        nc.sync.dma_start(given_list[:], offs3)
        nc.sync.dma_start(place_list[:], offs4)

        given_rows, old_rows, placed = [], [], []
        for r in range(ROW_TILES):
            g = sb.tile([P, Z], F32, name=f"given_rows{r}")
            nc.sync.dma_start(g[:], given[r * P : (r + 1) * P, :])
            given_rows.append(g)
        for r in range(ROW_TILES):
            o = sb.tile([P, M], F32, name=f"old_rows{r}")
            nc.sync.dma_start(o[:], old[r * P : (r + 1) * P, :])
            old_rows.append(o)
        for r in range(ROW_TILES):
            z = sb.tile([P, M], F32, name=f"placed{r}")
            nc.vector.memset(z[:], 0.0)
            placed.append(z)

        def vector_gather(dst, window, offsets):
            nc.vector.tensor_copy(dst, window[:].indirect(offsets))

        def scalar_gather(dst, window, offsets):
            nc.scalar.activation(dst, window[:].indirect(offsets), COPY)

        halves = [slice(0, HALF), slice(HALF, 2 * HALF)]
        list_halves = [slice(0, HALF // 16), slice(HALF // 16, 2 * HALF // 16)]

        picked_notes = sb.tile([P, PACK, J], BF16, name="picked_notes", align_bytes=64)
        key_scales = sb.tile([P, I], U8, name="key_scales", align_bytes=64)
        scalar_gather(picked_notes[:, 0, :], note_planes[0], note_list[:])
        vector_gather(key_scales[:], pool_scales, key_list[:])
        for t in range(1, PACK):
            vector_gather(picked_notes[:, t, halves[0]], note_planes[t], note_list[:, list_halves[0]])
            scalar_gather(picked_notes[:, t, halves[1]], note_planes[t], note_list[:, list_halves[1]])

        woven = sb.tile([P, J, PACK], BF16, name="woven", align_bytes=64)
        for h in halves:
            nc.vector.tensor_copy(
                woven[:, h, :].rearrange("p (c i) t -> p c t i", i=4),
                picked_notes[:, :, h].rearrange("p t (c i) -> p c t i", i=4),
            )
        note_words = sb.tile([P, J], U32, name="note_words", align_bytes=64)
        note_scales = sb.tile([P, J], U8, name="note_scales", align_bytes=64)
        for h in halves:
            nc.vector.quantize_mx(
                out=note_words[:, h].bitcast(FP8X4),
                scales=note_scales[:, h],
                in_=woven[:, h, :].rearrange("p j t -> p (j t)"),
            )

        first_words = sb.tile([P, P], U32, name="first_words", align_bytes=64)
        later_words = sb.tile([P, I - P], U32, name="later_words", align_bytes=64)
        vector_gather(first_words[:], pool_words, key_list[:, : P // 16])
        vector_gather(later_words[:], pool_words, key_list[:, P // 16 :])
        key_words = [first_words[:]] + [later_words[:, r * P : (r + 1) * P] for r in range(ROW_TILES - 1)]

        for r in range(ROW_TILES):
            rows = slice(r * P, (r + 1) * P)
            last = r == ROW_TILES - 1
            products = psum.tile([P, J], F32, name=f"products{r}")
            nc.tensor.matmul_mx(
                out=products[:],
                lhsT=key_words[r].bitcast(FP8X4),
                lhsT_scale=key_scales[:, rows],
                rhs=note_words[:].bitcast(FP8X4),
                rhs_scale=note_scales[:],
                start=True,
                stop=True,
            )
            picked_given = sb.tile([P, J], F32, name=f"picked_given{r}")
            if r == 0:
                vector_gather(picked_given[:, halves[0]], given_rows[r], given_list[:, list_halves[0]])
                scalar_gather(picked_given[:, halves[1]], given_rows[r], given_list[:, list_halves[1]])
            elif last:
                for h in range(2):
                    scalar_gather(picked_given[:, halves[h]], given_rows[r], given_list[:, list_halves[h]])
            else:
                scalar_gather(picked_given[:], given_rows[r], given_list[:])
            table = sb.tile([P, J], F32, name=f"table{r}")
            largest = sb.tile([P, N], F32, name=f"largest{r}")
            for cols in halves:
                nc.vector.tensor_tensor(table[:, cols], products[:, cols], picked_given[:, cols], ALU.mult)
            for cols in halves:
                nc.vector.tensor_reduce(
                    largest[:, cols.start // RUN : cols.stop // RUN],
                    table[:, cols].rearrange("p (n j) -> p n j", j=RUN),
                    mybir.AxisListType.X,
                    ALU.max,
                )
            nc.scalar.activation(placed[r][:].indirect(place_list[:]), largest[:], COPY)
            result = sb.tile([P, M], F32, name=f"result{r}")
            adder = nc.gpsimd if r < 2 else nc.vector
            adder.tensor_tensor(result[:], old_rows[r][:], placed[r][:], ALU.add)
            nc.sync.dma_start(out[rows, :], result[:])
